import numpy as np
import ml_dtypes


def mxq(x, axis, fmt="e4m3"):
    dtype, down = {"e4m3": (ml_dtypes.float8_e4m3fn, 7), "e5m2": (ml_dtypes.float8_e5m2, 14)}[fmt]
    v = np.moveaxis(np.asarray(x, np.float32).astype(ml_dtypes.bfloat16).astype(np.float64), axis, -1)
    blocks = v.reshape(v.shape[:-1] + (-1, 32))
    amax = np.abs(blocks).max(-1, keepdims=True)
    byte = np.maximum(np.where(amax > 0, np.frexp(amax)[1] - 1 + 127, 0) - down, 1)
    scale = np.exp2(byte - 127.0)
    codes = (blocks / scale).astype(np.float32).astype(dtype).astype(np.float64)
    return np.moveaxis((codes * scale).reshape(v.shape), -1, axis)


WIDE = False


def mx_kscale(k):
    if not WIDE:
        return np.ones(k)
    levels = np.array([30, -30])
    if k % 512:
        return np.exp2(np.random.permutation(np.resize(levels, k // 32))).repeat(32)
    a = np.empty((k // 512, 16))
    for p in range(k // 512):
        a[p, :8] = np.random.permutation(np.resize(levels, 8))
        for g in range(8):
            far = levels[np.abs(levels - a[p, g]) >= 10]
            a[p, g + 8] = far[np.random.randint(len(far))]
    return np.exp2(a.ravel()).repeat(32)


def f64(x):
    return np.asarray(x).astype(np.float64)


def striped(idx):
    return np.tile(np.asarray(idx).reshape(-1, 16).T, (8, 1)).astype(np.uint16)


def unstriped(offs):
    return offs[:16].T.reshape(-1).astype(np.int64)


E2M1 = np.array([0.0, 0.5, 1.0, 1.5, 2.0, 3.0, 4.0, 6.0, -0.0, -0.5, -1.0, -1.5, -2.0, -3.0, -4.0, -6.0])


def pack_weight(w, fmt):
    k, n = w.shape
    w = f64(np.asarray(w, np.float32).astype(ml_dtypes.bfloat16)).reshape(k // 32, 32, n)
    amax = np.abs(w).max(1)
    if fmt in ("e4m3", "e5m2"):
        byte = np.frexp(amax)[1] - 1 + 127 - (7 if fmt == "e4m3" else 14)
    else:
        mant, ex = np.frexp(amax / 6.0)
        byte = np.where(mant > 0.5, ex, ex - 1) + 127
    byte = np.clip(np.where(amax > 0, byte, 1), 1, 254)
    scaled = (w * np.exp2(127.0 - byte)[:, None, :]).reshape(k, n).astype(np.float32)
    by_word = np.ascontiguousarray(scaled.reshape(k // 512, 128, 4, n).transpose(0, 1, 3, 2))
    if fmt in ("e4m3", "e5m2"):
        words = by_word.astype(ml_dtypes.float8_e4m3fn if fmt == "e4m3" else ml_dtypes.float8_e5m2).view(np.uint8)
    else:
        c = by_word.astype(ml_dtypes.float4_e2m1fn).view(np.uint8) & 0xF
        words = (c[..., 0::2] | (c[..., 1::2] << 4)).reshape(k // 512, 128, 2 * n)
    return np.ascontiguousarray(words), np.ascontiguousarray(byte.astype(np.uint8).reshape(k // 512, 16, n))


def unpack_weight(words, scales, fmt):
    g, _, n = scales.shape
    words = np.ascontiguousarray(words).reshape(g, 128, n, -1)
    if fmt in ("e4m3", "e5m2"):
        vals = words.view(ml_dtypes.float8_e4m3fn if fmt == "e4m3" else ml_dtypes.float8_e5m2).astype(np.float64)
    else:
        nib = np.empty((g, 128, n, 4), np.uint8)
        nib[..., 0::2] = words & 0xF
        nib[..., 1::2] = words >> 4
        vals = E2M1[nib]
    vals = vals * np.repeat(np.exp2(scales.astype(np.float64) - 127.0), 8, axis=1)[..., None]
    return vals.transpose(0, 1, 3, 2).reshape(g * 512, n)


def bf(x):
    return np.asarray(x, np.float32).astype(ml_dtypes.bfloat16)


def planes(Y):
    r, m = Y.shape
    b = f64(bf(Y)).reshape(r // 32, 32, m)
    amax = np.abs(b).max(1)
    byte = np.clip(np.where(amax > 0, np.frexp(amax)[1] - 1 + 127 - 7, 1), 1, 254)
    codes = (b * np.exp2(127.0 - byte)[:, None, :]).reshape(r, m).astype(np.float32).astype(ml_dtypes.float8_e4m3fn).view(np.uint8)
    words = codes.reshape(r // 512, 128, 4, m).transpose(0, 1, 3, 2)
    return np.ascontiguousarray(words), np.ascontiguousarray(byte.astype(np.uint8).reshape(r // 512, 16, m))


K, T, J, S, R, F, Z, V, N = 512, 512, 256, 512, 512, 512, 1024, 512, 512


def setup_inputs():
    n = np.random.standard_normal
    idx = np.random.permutation(T)[:J]
    idx2 = np.random.permutation(S)[:J]
    idx3 = np.random.permutation(Z)[:J]
    idx4 = np.random.permutation(V)[:J]
    fk = mx_kscale(K)
    fr = mx_kscale(R)
    ff = mx_kscale(F)
    wp = pack_weight(n((K, R)) * 1 / np.sqrt(K) * fk[:, None] * fr, "e5m2")
    w2p = pack_weight(n((F, R)) * 1 / np.sqrt(F) * ff[:, None] * fr, "e4m3")
    wbp = pack_weight(n((R, N)) * 1 / np.sqrt(R) / fr[:, None], "e2m1")
    return {
        "xa": (n((K, T))).astype(np.float32),
        "xb": (n((K, S))).astype(np.float32),
        "hb": (np.random.uniform(0.2, 0.9, (K, 1))).astype(np.float32),
        "fk": (np.random.uniform(0.5, 2.0, (K, 1)) / fk[:, None]).astype(np.float32),
        "w_words": wp[0],
        "w_scales": wp[1],
        "xo": (n((F, Z))).astype(np.float32),
        "fl": (np.random.uniform(0.5, 2.0, (F, 1)) / ff[:, None]).astype(np.float32),
        "so": (n((F, J)) * 0.8).astype(np.float32),
        "w2_words": w2p[0],
        "w2_scales": w2p[1],
        "tb": (n((R, V)) * 0.7 * fr[:, None]).astype(np.float32),
        "wb_words": wbp[0],
        "wb_scales": wbp[1],
        "rs": (n((N, J))).astype(np.float32),
        "gm": (np.random.uniform(0.5, 2.0, (N, 1))).astype(np.float32),
        "offs": striped(idx),
        "offs2": striped(idx2),
        "offs3": striped(idx3),
        "offs4": striped(idx4),
    }


def reference(xa, xb, hb, fk, w_words, w_scales, xo, fl, so, w2_words, w2_scales, tb, wb_words, wb_scales, rs, gm, offs, offs2, offs3, offs4):
    idx = unstriped(offs)
    idx2 = unstriped(offs2)
    idx3 = unstriped(offs3)
    idx4 = unstriped(offs4)
    wu = unpack_weight(w_words, w_scales, "e5m2")
    w2u = unpack_weight(w2_words, w2_scales, "e4m3")
    wbu = unpack_weight(wb_words, wb_scales, "e2m1")
    u = (f64(xa)[:, idx] - np.minimum(f64(xb)[:, idx2], f64(hb))) * f64(fk)
    u2 = np.maximum(f64(xo)[:, idx3], f64(so)) * f64(fl)
    uq = mxq(u, 0, "e5m2")
    u2q = mxq(u2, 0, "e5m2")
    a = wu.T @ uq + w2u.T @ u2q
    hid = np.maximum(a, f64(tb)[:, idx4])
    hidq = mxq(hid, 0, "e5m2")
    p = wbu.T @ hidq
    y = f64(gm) * p + f64(rs)
    words, scales = planes(y)
    return y, words, scales

@@ -1,0 +1,207 @@
+from contextlib import ExitStack
+
+import concourse.mybir as mybir
+
+F32 = mybir.dt.float32
+BF16 = mybir.dt.bfloat16
+I32 = mybir.dt.int32
+U32 = mybir.dt.uint32
+U16 = mybir.dt.uint16
+U8 = mybir.dt.uint8
+E4M3 = mybir.dt.float8_e4m3fn_x4
+E5M2 = mybir.dt.float8_e5m2_x4
+E2M1 = mybir.dt.float4_e2m1fn_x4
+ALU = mybir.AluOpType
+COPY = mybir.ActivationFunctionType.Copy
+
+P = 128
+PACK = 4
+D = 512
+J = 256
+HALF = 128
+RUN = 4
+
+FLOPS = 3 * 2 * D * D * J
+
+
+def tile_list_sum_boundedgaps_largest_abovetable_residual_pl_kernel(
+    tc, xa, xb, hb, fk, w_words, w_scales, xo, fl, so, w2_words, w2_scales, tb,
+    wb_words, wb_scales, rs, gm, offs, offs2, offs3, offs4, out_0, out_1, out_2,
+):
+    nc = tc.nc
+    with ExitStack() as ctx:
+        pool = ctx.enter_context(tc.tile_pool(name="held", bufs=1))
+        psum = ctx.enter_context(tc.psum_pool(name="psum", bufs=1))
+
+        def planes(x):
+            return x.rearrange("(p t) c -> p t c", t=PACK)
+
+        def load(name, shape, dtype, src):
+            tile = pool.tile(shape, dtype, name=name, align_bytes=64)
+            nc.sync.dma_start(out=tile[:], in_=src)
+            return tile
+
+        def load_list(name, src):
+            tile = pool.tile([P, J // 16], U16, name=name)
+            nc.sync.dma_start(tile[:], src)
+            return tile
+
+        def load_vec(name, src):
+            return load(name, [P, PACK], F32, src.rearrange("(p t) o -> p (t o)", t=PACK))
+
+        def load_words(name, src):
+            return load(name, [P, src.shape[1] // 4], I32, src.bitcast(I32))
+
+        raw_scales = pool.tile([P, 3, D], U8, name="raw_scales", align_bytes=64)
+        nc.gpsimd.memset(raw_scales[:].rearrange("p a c -> p (a c)").bitcast(I32), 0)
+
+        def load_scales(queue, a, src):
+            for q in range(4):
+                queue.dma_start(
+                    out=raw_scales[32 * q : 32 * q + 4, a, :].bitcast(I32),
+                    in_=src[0, 4 * q : 4 * q + 4, :].bitcast(I32),
+                )
+
+        load_scales(nc.gpsimd, 1, w_scales)
+        load_scales(nc.gpsimd, 2, wb_scales)
+
+        xo_p, xa_p, xb_p, tb_p = planes(xo), planes(xa), planes(xb), planes(tb)
+        l3 = load_list("l3", offs3)
+        xo_t = [load("xo0", [P, 1024], F32, xo_p[:, 0, :])]
+        w2_raw = load_words("w2_raw", w2_words[0].rearrange("p n t -> p (n t)"))
+        xo_t.append(load("xo1", [P, 1024], F32, xo_p[:, 1, :]))
+        load_scales(nc.sync, 0, w2_scales)
+        so_t = load("so_t", [P, PACK, J], F32, planes(so))
+        fl_t = load_vec("fl_t", fl)
+        xo_t.append(load("xo2", [P, 1024], F32, xo_p[:, 2, :]))
+        w_raw = load_words("w_raw", w_words[0].rearrange("p n t -> p (n t)"))
+        xo_t.append(load("xo3", [P, 1024], F32, xo_p[:, 3, :]))
+        l2 = load_list("l2", offs2)
+        hb_t = load_vec("hb_t", hb)
+        xb_t = [load(f"xb{h}", [P, 2, D], F32, xb_p[:, 2 * h : 2 * h + 2, :]) for h in range(2)]
+        fk_t = load_vec("fk_t", fk)
+        l1 = load_list("l1", offs)
+        xa_t = [load(f"xa{t}", [P, D], F32, xa_p[:, t, :]) for t in range(3)]
+        l4 = load_list("l4", offs4)
+        xa_t.append(load("xa3", [P, D], F32, xa_p[:, 3, :]))
+        tb_t = [load(f"tb{t}", [P, D], F32, tb_p[:, t, :]) for t in range(PACK)]
+        wb_raw = load_words("wb_raw", wb_words[0])
+        gm_t = load_vec("gm_t", gm)
+        rs_t = load("rs_t", [P, PACK, J], F32, planes(rs))
+
+        def deal(engine_copy, name, raw, dtype):
+            dealt = pool.tile([P, D], dtype, name=name, align_bytes=64)
+            engine_copy(
+                out=dealt[:].rearrange("p (t m) -> p t m", t=PACK),
+                in_=raw.rearrange("p (m t) -> p t m", t=PACK),
+            )
+            return dealt
+
+        def by_word(ap):
+            return ap.rearrange("p (c i) t -> p c t i", i=RUN)
+
+        def by_plane(ap):
+            return ap.rearrange("p t (c i) -> p c t i", i=RUN)
+
+        def spread(vec):
+            return vec[:].rearrange("p (c t i) -> p c t i", c=1, i=1).to_broadcast([P, HALF // RUN, PACK, RUN])
+
+        def half(h):
+            return slice(h * HALF, (h + 1) * HALF)
+
+        def quantize(name, grouped, fmt):
+            codes = pool.tile([P, HALF], U32, name=name + "_codes", align_bytes=64)
+            scales = pool.tile([P, HALF], U8, name=name + "_scales", align_bytes=64)
+            nc.vector.quantize_mx(out=codes[:].bitcast(fmt), scales=scales[:], in_=grouped[:].rearrange("p c t -> p (c t)"))
+            return codes, scales
+
+        w2_c = deal(nc.vector.tensor_copy, "w2_c", w2_raw[:].bitcast(U32), U32)
+        w2_s = deal(nc.vector.tensor_copy, "w2_s", raw_scales[:, 0, :], U8)
+        xo_g = pool.tile([P, PACK, J], F32, name="xo_g")
+        m2 = pool.tile([P, PACK, J], F32, name="m2")
+        for t in range(PACK):
+            nc.scalar.activation(xo_g[:, t, :], xo_t[t][:].indirect(l3[:]), COPY)
+            nc.vector.tensor_tensor(m2[:, t, :], xo_g[:, t, :], so_t[:, t, :], ALU.max)
+        w_c = deal(nc.vector.tensor_copy, "w_c", w_raw[:].bitcast(U32), U32)
+        w_s = deal(nc.vector.tensor_copy, "w_s", raw_scales[:, 1, :], U8)
+        u2_q = []
+        u2_b = [pool.tile([P, HALF, PACK], BF16, name=f"u2_b{h}", align_bytes=64) for h in range(2)]
+        for h in range(2):
+            nc.vector.tensor_tensor(by_word(u2_b[h][:]), by_plane(m2[:, :, half(h)]), spread(fl_t), ALU.mult)
+        for h in range(2):
+            u2_q.append(quantize(f"u2_{h}", u2_b[h], E5M2))
+
+
+        acc = [psum.tile([P, PACK, HALF], F32, name=f"acc{h}") for h in range(2)]
+        for h in range(2):
+            for t in range(PACK):
+                cols = slice(t * P, (t + 1) * P)
+                nc.tensor.matmul_mx(
+                    out=acc[h][:, t, :], lhsT=w2_c[:, cols].bitcast(E4M3), lhsT_scale=w2_s[:, cols],
+                    rhs=u2_q[h][0][:].bitcast(E5M2), rhs_scale=u2_q[h][1][:], start=(t == 0), stop=False,
+                )
+
+        xb_g = pool.tile([P, PACK, J], F32, name="xb_g")
+        low = pool.tile([P, PACK, J], F32, name="low")
+        for t in range(PACK):
+            nc.scalar.activation(xb_g[:, t, :], xb_t[t // 2][:, t % 2, :].indirect(l2[:]), COPY)
+            nc.vector.tensor_scalar(low[:, t, :], xb_g[:, t, :], hb_t[:, t : t + 1], None, ALU.min)
+        wb_s = deal(nc.vector.tensor_copy, "wb_s", raw_scales[:, 2, :], U8)
+        gap = pool.tile([P, PACK, J], F32, name="gap")
+        for t in range(PACK):
+            nc.vector.tensor_tensor(gap[:, t, :], xa_t[t][:].indirect(l1[:]), low[:, t, :], ALU.subtract)
+        u_b = [pool.tile([P, HALF, PACK], BF16, name=f"u_b{h}", align_bytes=64) for h in range(2)]
+        for h in range(2):
+            nc.vector.tensor_tensor(by_word(u_b[h][:]), by_plane(gap[:, :, half(h)]), spread(fk_t), ALU.mult)
+        for h in range(2):
+            codes, scales = quantize(f"u_{h}", u_b[h], E5M2)
+            for t in range(PACK):
+                cols = slice(t * P, (t + 1) * P)
+                nc.tensor.matmul_mx(
+                    out=acc[h][:, t, :], lhsT=w_c[:, cols].bitcast(E5M2), lhsT_scale=w_s[:, cols],
+                    rhs=codes[:].bitcast(E5M2), rhs_scale=scales[:], start=False, stop=(t == PACK - 1),
+                )
+
+        tb_g = pool.tile([P, PACK, J], F32, name="tb_g")
+        for t in range(PACK):
+            nc.scalar.activation(tb_g[:, t, :], tb_t[t][:].indirect(l4[:]), COPY)
+        wb_c = deal(nc.scalar.copy, "wb_c", wb_raw[:].bitcast(U16), U16)
+        hid_b = [pool.tile([P, HALF, PACK], BF16, name=f"hid_b{h}", align_bytes=64) for h in range(2)]
+        res = [psum.tile([P, PACK, HALF], F32, name=f"res{h}") for h in range(2)]
+        for h in range(2):
+            nc.vector.tensor_tensor(by_word(hid_b[h][:]), by_plane(acc[h][:]), by_plane(tb_g[:, :, half(h)]), ALU.max)
+        for h in range(2):
+            codes, scales = quantize(f"hid_{h}", hid_b[h], E5M2)
+            for t in range(PACK):
+                cols = slice(t * P, (t + 1) * P)
+                nc.tensor.matmul_mx(
+                    out=res[h][:, t, :], lhsT=wb_c[:, cols].bitcast(E2M1), lhsT_scale=wb_s[:, cols],
+                    rhs=codes[:].bitcast(E5M2), rhs_scale=scales[:], start=True, stop=True,
+                )
+
+        y_codes = pool.tile([P, J], U32, name="y_codes", align_bytes=64)
+        y_scales = pool.tile([P, J], U8, name="y_scales", align_bytes=64)
+        out_p = planes(out_0)
+        words_out = out_1[0].rearrange("p c t -> p (c t)").bitcast(I32)
+        y = [pool.tile([P, PACK, HALF], F32, name=f"y{h}") for h in range(2)]
+        y_b = [pool.tile([P, HALF, PACK], BF16, name=f"y_b{h}", align_bytes=64) for h in range(2)]
+        for h in range(2):
+            for t in range(PACK):
+                nc.vector.scalar_tensor_tensor(
+                    y[h][:, t, :], res[h][:, t, :], gm_t[:, t : t + 1], rs_t[:, t, half(h)], ALU.mult, ALU.add
+                )
+            nc.sync.dma_start(out=out_p[:, :, half(h)], in_=y[h][:])
+        nc.scalar.copy(out=by_word(y_b[0][:]), in_=by_plane(y[0][:]))
+        nc.vector.tensor_copy(out=by_word(y_b[1][:]), in_=by_plane(y[1][:]))
+        for h in range(2):
+            nc.vector.quantize_mx(
+                out=y_codes[:, half(h)].bitcast(E4M3), scales=y_scales[:, half(h)],
+                in_=y_b[h][:].rearrange("p c t -> p (c t)"),
+            )
+        nc.scalar.dma_start(out=words_out, in_=y_codes[:].bitcast(I32))
+        for q in range(4):
+            queue = nc.sync if q % 2 == 0 else nc.scalar
+            queue.dma_start(
+                out=out_2[0, 4 * q : 4 * q + 4, :].bitcast(I32),
+                in_=y_scales[32 * q : 32 * q + 4, :].bitcast(I32),
+            )

@@ -52,41 +52,46 @@ def tile_list_sum_boundedgaps_largest_abovetable_residual_pl_kernel(
         def load_words(name, src):
             return load(name, [P, src.shape[1] // 4], I32, src.bitcast(I32))
 
-        raw_scales = pool.tile([P, 3, D], U8, name="raw_scales", align_bytes=64)
-        nc.gpsimd.memset(raw_scales[:].rearrange("p a c -> p (a c)").bitcast(I32), 0)
+        def scale_tile(name):
+            tile = pool.tile([P, D], U8, name=name, align_bytes=64)
+            nc.gpsimd.memset(tile[:].bitcast(I32), 0)
+            return tile
 
-        def load_scales(queue, a, src):
-            for q in range(4):
+        def load_scales(queue, tile, src, quadrants):
+            for q in quadrants:
                 queue.dma_start(
-                    out=raw_scales[32 * q : 32 * q + 4, a, :].bitcast(I32),
+                    out=tile[32 * q : 32 * q + 4, :].bitcast(I32),
                     in_=src[0, 4 * q : 4 * q + 4, :].bitcast(I32),
                 )
 
-        load_scales(nc.gpsimd, 1, w_scales)
-        load_scales(nc.gpsimd, 2, wb_scales)
+        w2_sraw, w_sraw, wb_sraw = scale_tile("w2_sraw"), scale_tile("w_sraw"), scale_tile("wb_sraw")
+        load_scales(nc.gpsimd, wb_sraw, wb_scales, range(4))
+        gm_t = pool.tile([P, PACK], F32, name="gm_t", align_bytes=64)
+        nc.gpsimd.dma_start(out=gm_t[:], in_=gm.rearrange("(p t) o -> p (t o)", t=PACK))
 
         xo_p, xa_p, xb_p, tb_p = planes(xo), planes(xa), planes(xb), planes(tb)
+        l2 = load_list("l2", offs2)
+        xb_t = [load("xb0", [P, 2, D], F32, xb_p[:, 0:2, :])]
+        l1 = load_list("l1", offs)
+        xa_t = [load("xa0", [P, 2, D], F32, xa_p[:, 0:2, :])]
+        hb_t = load_vec("hb_t", hb)
+        fk_t = load_vec("fk_t", fk)
+        xb_t.append(load("xb1", [P, 2, D], F32, xb_p[:, 2:4, :]))
+        xa_t.append(load("xa1", [P, 2, D], F32, xa_p[:, 2:4, :]))
+        load_scales(nc.sync, w_sraw, w_scales, range(4))
+        w_raw = load_words("w_raw", w_words[0].rearrange("p n t -> p (n t)"))
+        w2_raw = load_words("w2_raw", w2_words[0].rearrange("p n t -> p (n t)"))
+        so_t = load("so_t", [P, PACK, J], F32, planes(so))
         l3 = load_list("l3", offs3)
         xo_t = [load("xo0", [P, 1024], F32, xo_p[:, 0, :])]
-        w2_raw = load_words("w2_raw", w2_words[0].rearrange("p n t -> p (n t)"))
-        xo_t.append(load("xo1", [P, 1024], F32, xo_p[:, 1, :]))
-        load_scales(nc.sync, 0, w2_scales)
-        so_t = load("so_t", [P, PACK, J], F32, planes(so))
         fl_t = load_vec("fl_t", fl)
+        xo_t.append(load("xo1", [P, 1024], F32, xo_p[:, 1, :]))
+        load_scales(nc.sync, w2_sraw, w2_scales, range(4))
         xo_t.append(load("xo2", [P, 1024], F32, xo_p[:, 2, :]))
-        w_raw = load_words("w_raw", w_words[0].rearrange("p n t -> p (n t)"))
-        xo_t.append(load("xo3", [P, 1024], F32, xo_p[:, 3, :]))
-        l2 = load_list("l2", offs2)
-        hb_t = load_vec("hb_t", hb)
-        xb_t = [load(f"xb{h}", [P, 2, D], F32, xb_p[:, 2 * h : 2 * h + 2, :]) for h in range(2)]
-        fk_t = load_vec("fk_t", fk)
-        l1 = load_list("l1", offs)
-        xa_t = [load(f"xa{t}", [P, D], F32, xa_p[:, t, :]) for t in range(3)]
         l4 = load_list("l4", offs4)
-        xa_t.append(load("xa3", [P, D], F32, xa_p[:, 3, :]))
+        xo_t.append(load("xo3", [P, 1024], F32, xo_p[:, 3, :]))
         tb_t = [load(f"tb{t}", [P, D], F32, tb_p[:, t, :]) for t in range(PACK)]
         wb_raw = load_words("wb_raw", wb_words[0])
-        gm_t = load_vec("gm_t", gm)
         rs_t = load("rs_t", [P, PACK, J], F32, planes(rs))
 
         def deal(engine_copy, name, raw, dtype):
@@ -112,70 +117,94 @@ def tile_list_sum_boundedgaps_largest_abovetable_residual_pl_kernel(
         def quantize(name, grouped, fmt):
             codes = pool.tile([P, HALF], U32, name=name + "_codes", align_bytes=64)
             scales = pool.tile([P, HALF], U8, name=name + "_scales", align_bytes=64)
-            nc.vector.quantize_mx(out=codes[:].bitcast(fmt), scales=scales[:], in_=grouped[:].rearrange("p c t -> p (c t)"))
+            nc.vector.quantize_mx(out=codes[:].bitcast(fmt), scales=scales[:], in_=grouped.rearrange("p c t -> p (c t)"))
             return codes, scales
 
-        w2_c = deal(nc.vector.tensor_copy, "w2_c", w2_raw[:].bitcast(U32), U32)
-        w2_s = deal(nc.vector.tensor_copy, "w2_s", raw_scales[:, 0, :], U8)
-        xo_g = pool.tile([P, PACK, J], F32, name="xo_g")
-        m2 = pool.tile([P, PACK, J], F32, name="m2")
-        for t in range(PACK):
-            nc.scalar.activation(xo_g[:, t, :], xo_t[t][:].indirect(l3[:]), COPY)
-            nc.vector.tensor_tensor(m2[:, t, :], xo_g[:, t, :], so_t[:, t, :], ALU.max)
-        w_c = deal(nc.vector.tensor_copy, "w_c", w_raw[:].bitcast(U32), U32)
-        w_s = deal(nc.vector.tensor_copy, "w_s", raw_scales[:, 1, :], U8)
-        u2_q = []
-        u2_b = [pool.tile([P, HALF, PACK], BF16, name=f"u2_b{h}", align_bytes=64) for h in range(2)]
-        for h in range(2):
-            nc.vector.tensor_tensor(by_word(u2_b[h][:]), by_plane(m2[:, :, half(h)]), spread(fl_t), ALU.mult)
-        for h in range(2):
-            u2_q.append(quantize(f"u2_{h}", u2_b[h], E5M2))
+        def gather_s(dst, window, offsets):
+            nc.scalar.activation(dst, window.indirect(offsets), COPY)
 
+        def gather_v(dst, window, offsets):
+            nc.vector.tensor_copy(dst, window.indirect(offsets))
 
-        acc = [psum.tile([P, PACK, HALF], F32, name=f"acc{h}") for h in range(2)]
-        for h in range(2):
-            for t in range(PACK):
-                cols = slice(t * P, (t + 1) * P)
-                nc.tensor.matmul_mx(
-                    out=acc[h][:, t, :], lhsT=w2_c[:, cols].bitcast(E4M3), lhsT_scale=w2_s[:, cols],
-                    rhs=u2_q[h][0][:].bitcast(E5M2), rhs_scale=u2_q[h][1][:], start=(t == 0), stop=False,
-                )
+        def half_list(lst, h):
+            return lst[:, h * (HALF // 16) : (h + 1) * (HALF // 16)]
 
+        fk_neg = pool.tile([P, PACK], F32, name="fk_neg", align_bytes=64)
+        nc.vector.tensor_scalar(fk_neg[:], fk_t[:], -1.0, None, ALU.mult)
         xb_g = pool.tile([P, PACK, J], F32, name="xb_g")
-        low = pool.tile([P, PACK, J], F32, name="low")
-        for t in range(PACK):
-            nc.scalar.activation(xb_g[:, t, :], xb_t[t // 2][:, t % 2, :].indirect(l2[:]), COPY)
-            nc.vector.tensor_scalar(low[:, t, :], xb_g[:, t, :], hb_t[:, t : t + 1], None, ALU.min)
-        wb_s = deal(nc.vector.tensor_copy, "wb_s", raw_scales[:, 2, :], U8)
+        xa_g = pool.tile([P, PACK, J], F32, name="xa_g")
         gap = pool.tile([P, PACK, J], F32, name="gap")
-        for t in range(PACK):
-            nc.vector.tensor_tensor(gap[:, t, :], xa_t[t][:].indirect(l1[:]), low[:, t, :], ALU.subtract)
+        for pair in range(2):
+            for dst, src, lst in ((xb_g, xb_t, l2), (xa_g, xa_t, l1)):
+                gather_s(dst[:, 2 * pair, :], src[pair][:, 0, :], lst[:])
+                gather_v(dst[:, 2 * pair + 1, :], src[pair][:, 1, :], lst[:])
+            for t in (2 * pair + 1, 2 * pair):
+                nc.vector.scalar_tensor_tensor(
+                    gap[:, t, :], xb_g[:, t, :], hb_t[:, t : t + 1], xa_g[:, t, :], ALU.min, ALU.subtract
+                )
+        w_s = deal(nc.gpsimd.tensor_copy, "w_s", w_sraw[:], U8)
+        wb_s = deal(nc.gpsimd.tensor_copy, "wb_s", wb_sraw[:], U8)
+        w2_s = deal(nc.gpsimd.tensor_copy, "w2_s", w2_sraw[:], U8)
+        w_c = deal(nc.scalar.copy, "w_c", w_raw[:].bitcast(U32), U32)
+        w2_c = deal(nc.scalar.copy, "w2_c", w2_raw[:].bitcast(U32), U32)
         u_b = [pool.tile([P, HALF, PACK], BF16, name=f"u_b{h}", align_bytes=64) for h in range(2)]
         for h in range(2):
-            nc.vector.tensor_tensor(by_word(u_b[h][:]), by_plane(gap[:, :, half(h)]), spread(fk_t), ALU.mult)
+            nc.vector.tensor_tensor(by_word(u_b[h][:]), by_plane(gap[:, :, half(h)]), spread(fk_neg), ALU.mult)
+        acc = [psum.tile([P, PACK, HALF], F32, name=f"acc{h}") for h in range(2)]
         for h in range(2):
-            codes, scales = quantize(f"u_{h}", u_b[h], E5M2)
+            codes, scales = quantize(f"u_{h}", u_b[h][:], E5M2)
             for t in range(PACK):
                 cols = slice(t * P, (t + 1) * P)
                 nc.tensor.matmul_mx(
                     out=acc[h][:, t, :], lhsT=w_c[:, cols].bitcast(E5M2), lhsT_scale=w_s[:, cols],
+                    rhs=codes[:].bitcast(E5M2), rhs_scale=scales[:], start=(t == 0), stop=False,
+                )
+
+        xo_g = pool.tile([P, PACK, J], F32, name="xo_g")
+        m2 = pool.tile([P, PACK, J], F32, name="m2")
+        u2_b = pool.tile([P, J, PACK], BF16, name="u2_b", align_bytes=64)
+
+        def larger(t, cols):
+            nc.vector.tensor_tensor(m2[:, t, cols], xo_g[:, t, cols], so_t[:, t, cols], ALU.max)
+
+        def scaled(t, cols):
+            nc.vector.tensor_scalar(u2_b[:, cols, t], m2[:, t, cols], fl_t[:, t : t + 1], None, ALU.mult)
+
+        for t in range(PACK - 1):
+            gather_s(xo_g[:, t, :], xo_t[t][:], l3[:])
+            larger(t, slice(0, J))
+            scaled(t, slice(0, J))
+        gather_v(xo_g[:, 3, half(0)], xo_t[3][:], half_list(l3, 0))
+        gather_s(xo_g[:, 3, half(1)], xo_t[3][:], half_list(l3, 1))
+        for h in range(2):
+            larger(3, half(h))
+        for h in range(2):
+            scaled(3, half(h))
+        for h in range(2):
+            codes, scales = quantize(f"u2_{h}", u2_b[:, half(h), :], E5M2)
+            for t in range(PACK):
+                cols = slice(t * P, (t + 1) * P)
+                nc.tensor.matmul_mx(
+                    out=acc[h][:, t, :], lhsT=w2_c[:, cols].bitcast(E4M3), lhsT_scale=w2_s[:, cols],
                     rhs=codes[:].bitcast(E5M2), rhs_scale=scales[:], start=False, stop=(t == PACK - 1),
                 )
 
         tb_g = pool.tile([P, PACK, J], F32, name="tb_g")
-        for t in range(PACK):
-            nc.scalar.activation(tb_g[:, t, :], tb_t[t][:].indirect(l4[:]), COPY)
+        for t in range(PACK - 1):
+            gather = gather_v if t == 2 else gather_s
+            gather(tb_g[:, t, :], tb_t[t][:], l4[:])
+        for h in range(2):
+            gather_s(tb_g[:, 3, half(h)], tb_t[3][:], half_list(l4, h))
         wb_c = deal(nc.scalar.copy, "wb_c", wb_raw[:].bitcast(U16), U16)
         hid_b = [pool.tile([P, HALF, PACK], BF16, name=f"hid_b{h}", align_bytes=64) for h in range(2)]
-        res = [psum.tile([P, PACK, HALF], F32, name=f"res{h}") for h in range(2)]
+        res = [[psum.tile([P, 2, HALF], F32, name=f"res{h}{b}") for b in range(2)] for h in range(2)]
         for h in range(2):
             nc.vector.tensor_tensor(by_word(hid_b[h][:]), by_plane(acc[h][:]), by_plane(tb_g[:, :, half(h)]), ALU.max)
-        for h in range(2):
-            codes, scales = quantize(f"hid_{h}", hid_b[h], E5M2)
+            codes, scales = quantize(f"hid_{h}", hid_b[h][:], E5M2)
             for t in range(PACK):
                 cols = slice(t * P, (t + 1) * P)
                 nc.tensor.matmul_mx(
-                    out=res[h][:, t, :], lhsT=wb_c[:, cols].bitcast(E2M1), lhsT_scale=wb_s[:, cols],
+                    out=res[h][t // 2][:, t % 2, :], lhsT=wb_c[:, cols].bitcast(E2M1), lhsT_scale=wb_s[:, cols],
                     rhs=codes[:].bitcast(E5M2), rhs_scale=scales[:], start=True, stop=True,
                 )
 
@@ -188,7 +217,7 @@ def tile_list_sum_boundedgaps_largest_abovetable_residual_pl_kernel(
         for h in range(2):
             for t in range(PACK):
                 nc.vector.scalar_tensor_tensor(
-                    y[h][:, t, :], res[h][:, t, :], gm_t[:, t : t + 1], rs_t[:, t, half(h)], ALU.mult, ALU.add
+                    y[h][:, t, :], res[h][t // 2][:, t % 2, :], gm_t[:, t : t + 1], rs_t[:, t, half(h)], ALU.mult, ALU.add
                 )
             nc.sync.dma_start(out=out_p[:, :, half(h)], in_=y[h][:])
         nc.scalar.copy(out=by_word(y_b[0][:]), in_=by_plane(y[0][:]))

@@ -36,9 +36,9 @@ def tile_list_sum_boundedgaps_largest_abovetable_residual_pl_kernel(
         def planes(x):
             return x.rearrange("(p t) c -> p t c", t=PACK)
 
-        def load(name, shape, dtype, src):
+        def load(name, shape, dtype, src, queue=nc.sync):
             tile = pool.tile(shape, dtype, name=name, align_bytes=64)
-            nc.sync.dma_start(out=tile[:], in_=src)
+            queue.dma_start(out=tile[:], in_=src)
             return tile
 
         def load_list(name, src):
@@ -46,8 +46,8 @@ def tile_list_sum_boundedgaps_largest_abovetable_residual_pl_kernel(
             nc.sync.dma_start(tile[:], src)
             return tile
 
-        def load_vec(name, src):
-            return load(name, [P, PACK], F32, src.rearrange("(p t) o -> p (t o)", t=PACK))
+        def load_vec(name, src, queue=nc.sync):
+            return load(name, [P, PACK], F32, src.rearrange("(p t) o -> p (t o)", t=PACK), queue)
 
         def load_words(name, src):
             return load(name, [P, src.shape[1] // 4], I32, src.bitcast(I32))
@@ -65,33 +65,34 @@ def tile_list_sum_boundedgaps_largest_abovetable_residual_pl_kernel(
                 )
 
         w2_sraw, w_sraw, wb_sraw = scale_tile("w2_sraw"), scale_tile("w_sraw"), scale_tile("wb_sraw")
+        load_scales(nc.gpsimd, w_sraw, w_scales, range(4))
         load_scales(nc.gpsimd, wb_sraw, wb_scales, range(4))
-        gm_t = pool.tile([P, PACK], F32, name="gm_t", align_bytes=64)
-        nc.gpsimd.dma_start(out=gm_t[:], in_=gm.rearrange("(p t) o -> p (t o)", t=PACK))
 
-        xo_p, xa_p, xb_p, tb_p = planes(xo), planes(xa), planes(xb), planes(tb)
+        xo_p, tb_p = planes(xo), planes(tb)
+        xa_p, xb_p = planes(xa), planes(xb)
+        fk_t = load_vec("fk_t", fk, nc.scalar)
+        hb_t = load_vec("hb_t", hb, nc.scalar)
+        xb_t = [load("xb_01", [P, 2, D], F32, xb_p[:, 0:2, :])]
         l2 = load_list("l2", offs2)
-        xb_t = [load("xb0", [P, 2, D], F32, xb_p[:, 0:2, :])]
+        xa_t = [load("xa_01", [P, 2, D], F32, xa_p[:, 0:2, :])]
         l1 = load_list("l1", offs)
-        xa_t = [load("xa0", [P, 2, D], F32, xa_p[:, 0:2, :])]
-        hb_t = load_vec("hb_t", hb)
-        fk_t = load_vec("fk_t", fk)
-        xb_t.append(load("xb1", [P, 2, D], F32, xb_p[:, 2:4, :]))
-        xa_t.append(load("xa1", [P, 2, D], F32, xa_p[:, 2:4, :]))
-        load_scales(nc.sync, w_sraw, w_scales, range(4))
-        w_raw = load_words("w_raw", w_words[0].rearrange("p n t -> p (n t)"))
-        w2_raw = load_words("w2_raw", w2_words[0].rearrange("p n t -> p (n t)"))
+        xb_t.append(load("xb_23", [P, 2, D], F32, xb_p[:, 2:4, :]))
+        xa_t.append(load("xa_23", [P, 2, D], F32, xa_p[:, 2:4, :]))
         so_t = load("so_t", [P, PACK, J], F32, planes(so))
+        load_scales(nc.sync, w2_sraw, w2_scales, range(2))
+        xo_01 = load("xo_01", [P, 2, 1024], F32, xo_p[:, 0:2, :])
         l3 = load_list("l3", offs3)
-        xo_t = [load("xo0", [P, 1024], F32, xo_p[:, 0, :])]
         fl_t = load_vec("fl_t", fl)
-        xo_t.append(load("xo1", [P, 1024], F32, xo_p[:, 1, :]))
-        load_scales(nc.sync, w2_sraw, w2_scales, range(4))
-        xo_t.append(load("xo2", [P, 1024], F32, xo_p[:, 2, :]))
+        load_scales(nc.sync, w2_sraw, w2_scales, range(2, 4))
+        xo_2 = load("xo_2", [P, 1024], F32, xo_p[:, 2, :])
+        w2_raw = load_words("w2_raw", w2_words[0].rearrange("p n t -> p (n t)"))
+        xo_3 = load("xo_3", [P, 1024], F32, xo_p[:, 3, :])
+        w_raw = load_words("w_raw", w_words[0].rearrange("p n t -> p (n t)"))
+        xo_t = [xo_01[:, 0, :], xo_01[:, 1, :], xo_2[:], xo_3[:]]
         l4 = load_list("l4", offs4)
-        xo_t.append(load("xo3", [P, 1024], F32, xo_p[:, 3, :]))
         tb_t = [load(f"tb{t}", [P, D], F32, tb_p[:, t, :]) for t in range(PACK)]
         wb_raw = load_words("wb_raw", wb_words[0])
+        gm_t = load_vec("gm_t", gm)
         rs_t = load("rs_t", [P, PACK, J], F32, planes(rs))
 
         def deal(engine_copy, name, raw, dtype):
@@ -130,7 +131,7 @@ def tile_list_sum_boundedgaps_largest_abovetable_residual_pl_kernel(
             return lst[:, h * (HALF // 16) : (h + 1) * (HALF // 16)]
 
         fk_neg = pool.tile([P, PACK], F32, name="fk_neg", align_bytes=64)
-        nc.vector.tensor_scalar(fk_neg[:], fk_t[:], -1.0, None, ALU.mult)
+        nc.scalar.activation(fk_neg[:], fk_t[:], COPY, scale=-1.0)
         xb_g = pool.tile([P, PACK, J], F32, name="xb_g")
         xa_g = pool.tile([P, PACK, J], F32, name="xa_g")
         gap = pool.tile([P, PACK, J], F32, name="gap")
@@ -143,22 +144,13 @@ def tile_list_sum_boundedgaps_largest_abovetable_residual_pl_kernel(
                     gap[:, t, :], xb_g[:, t, :], hb_t[:, t : t + 1], xa_g[:, t, :], ALU.min, ALU.subtract
                 )
         w_s = deal(nc.gpsimd.tensor_copy, "w_s", w_sraw[:], U8)
-        wb_s = deal(nc.gpsimd.tensor_copy, "wb_s", wb_sraw[:], U8)
         w2_s = deal(nc.gpsimd.tensor_copy, "w2_s", w2_sraw[:], U8)
-        w_c = deal(nc.scalar.copy, "w_c", w_raw[:].bitcast(U32), U32)
-        w2_c = deal(nc.scalar.copy, "w2_c", w2_raw[:].bitcast(U32), U32)
+        wb_s = deal(nc.gpsimd.tensor_copy, "wb_s", wb_sraw[:], U8)
         u_b = [pool.tile([P, HALF, PACK], BF16, name=f"u_b{h}", align_bytes=64) for h in range(2)]
         for h in range(2):
             nc.vector.tensor_tensor(by_word(u_b[h][:]), by_plane(gap[:, :, half(h)]), spread(fk_neg), ALU.mult)
+        u_q = [quantize(f"u_{h}", u_b[h][:], E5M2) for h in range(2)]
         acc = [psum.tile([P, PACK, HALF], F32, name=f"acc{h}") for h in range(2)]
-        for h in range(2):
-            codes, scales = quantize(f"u_{h}", u_b[h][:], E5M2)
-            for t in range(PACK):
-                cols = slice(t * P, (t + 1) * P)
-                nc.tensor.matmul_mx(
-                    out=acc[h][:, t, :], lhsT=w_c[:, cols].bitcast(E5M2), lhsT_scale=w_s[:, cols],
-                    rhs=codes[:].bitcast(E5M2), rhs_scale=scales[:], start=(t == 0), stop=False,
-                )
 
         xo_g = pool.tile([P, PACK, J], F32, name="xo_g")
         m2 = pool.tile([P, PACK, J], F32, name="m2")
@@ -171,11 +163,24 @@ def tile_list_sum_boundedgaps_largest_abovetable_residual_pl_kernel(
             nc.vector.tensor_scalar(u2_b[:, cols, t], m2[:, t, cols], fl_t[:, t : t + 1], None, ALU.mult)
 
         for t in range(PACK - 1):
-            gather_s(xo_g[:, t, :], xo_t[t][:], l3[:])
+            gather = gather_v if t == 1 else gather_s
+            gather(xo_g[:, t, :], xo_t[t], l3[:])
+        for t in (1, 0, 2):
             larger(t, slice(0, J))
             scaled(t, slice(0, J))
-        gather_v(xo_g[:, 3, half(0)], xo_t[3][:], half_list(l3, 0))
-        gather_s(xo_g[:, 3, half(1)], xo_t[3][:], half_list(l3, 1))
+        w2_c = deal(nc.scalar.copy, "w2_c", w2_raw[:].bitcast(U32), U32)
+        gather_v(xo_g[:, 3, half(0)], xo_t[3], half_list(l3, 0))
+        gather_s(xo_g[:, 3, half(1)], xo_t[3], half_list(l3, 1))
+        w_c = deal(nc.scalar.copy, "w_c", w_raw[:].bitcast(U32), U32)
+        for h in range(2):
+            codes, scales = u_q[h]
+            for t in range(PACK):
+                cols = slice(t * P, (t + 1) * P)
+                nc.tensor.matmul_mx(
+                    out=acc[h][:, t, :], lhsT=w_c[:, cols].bitcast(E5M2), lhsT_scale=w_s[:, cols],
+                    rhs=codes[:].bitcast(E5M2), rhs_scale=scales[:], start=(t == 0), stop=False,
+                )
+
         for h in range(2):
             larger(3, half(h))
         for h in range(2):
@@ -221,13 +226,14 @@ def tile_list_sum_boundedgaps_largest_abovetable_residual_pl_kernel(
                 )
             nc.sync.dma_start(out=out_p[:, :, half(h)], in_=y[h][:])
         nc.scalar.copy(out=by_word(y_b[0][:]), in_=by_plane(y[0][:]))
-        nc.vector.tensor_copy(out=by_word(y_b[1][:]), in_=by_plane(y[1][:]))
         for h in range(2):
+            if h == 1:
+                nc.vector.tensor_copy(out=by_word(y_b[1][:]), in_=by_plane(y[1][:]))
             nc.vector.quantize_mx(
                 out=y_codes[:, half(h)].bitcast(E4M3), scales=y_scales[:, half(h)],
                 in_=y_b[h][:].rearrange("p c t -> p (c t)"),
             )
-        nc.scalar.dma_start(out=words_out, in_=y_codes[:].bitcast(I32))
+            nc.scalar.dma_start(out=words_out[:, half(h)], in_=y_codes[:, half(h)].bitcast(I32))
         for q in range(4):
             queue = nc.sync if q % 2 == 0 else nc.scalar
             queue.dma_start(

from contextlib import ExitStack

import concourse.mybir as mybir

F32 = mybir.dt.float32
BF16 = mybir.dt.bfloat16
I32 = mybir.dt.int32
U32 = mybir.dt.uint32
U16 = mybir.dt.uint16
U8 = mybir.dt.uint8
E4M3 = mybir.dt.float8_e4m3fn_x4
E5M2 = mybir.dt.float8_e5m2_x4
E2M1 = mybir.dt.float4_e2m1fn_x4
ALU = mybir.AluOpType
COPY = mybir.ActivationFunctionType.Copy

P = 128
PACK = 4
D = 512
J = 256
HALF = 128
RUN = 4

FLOPS = 3 * 2 * D * D * J


def tile_list_sum_boundedgaps_largest_abovetable_residual_pl_kernel(
    tc, xa, xb, hb, fk, w_words, w_scales, xo, fl, so, w2_words, w2_scales, tb,
    wb_words, wb_scales, rs, gm, offs, offs2, offs3, offs4, out_0, out_1, out_2,
):
    nc = tc.nc
    with ExitStack() as ctx:
        pool = ctx.enter_context(tc.tile_pool(name="held", bufs=1))
        psum = ctx.enter_context(tc.psum_pool(name="psum", bufs=1))

        def planes(x):
            return x.rearrange("(p t) c -> p t c", t=PACK)

        def load(name, shape, dtype, src, queue=nc.sync):
            tile = pool.tile(shape, dtype, name=name, align_bytes=64)
            queue.dma_start(out=tile[:], in_=src)
            return tile

        def load_list(name, src):
            tile = pool.tile([P, J // 16], U16, name=name)
            nc.sync.dma_start(tile[:], src)
            return tile

        def load_vec(name, src, queue=nc.sync):
            return load(name, [P, PACK], F32, src.rearrange("(p t) o -> p (t o)", t=PACK), queue)

        def load_words(name, src):
            return load(name, [P, src.shape[1] // 4], I32, src.bitcast(I32))

        def scale_tile(name):
            tile = pool.tile([P, D], U8, name=name, align_bytes=64)
            nc.gpsimd.memset(tile[:].bitcast(I32), 0)
            return tile

        def load_scales(queue, tile, src, quadrants):
            for q in quadrants:
                queue.dma_start(
                    out=tile[32 * q : 32 * q + 4, :].bitcast(I32),
                    in_=src[0, 4 * q : 4 * q + 4, :].bitcast(I32),
                )

        w2_sraw, w_sraw, wb_sraw = scale_tile("w2_sraw"), scale_tile("w_sraw"), scale_tile("wb_sraw")
        load_scales(nc.gpsimd, w_sraw, w_scales, range(4))
        load_scales(nc.gpsimd, wb_sraw, wb_scales, range(4))

        xo_p, tb_p = planes(xo), planes(tb)
        xa_p, xb_p = planes(xa), planes(xb)
        fk_t = load_vec("fk_t", fk, nc.scalar)
        hb_t = load_vec("hb_t", hb, nc.scalar)
        xb_t = [load("xb_01", [P, 2, D], F32, xb_p[:, 0:2, :])]
        l2 = load_list("l2", offs2)
        xa_t = [load("xa_01", [P, 2, D], F32, xa_p[:, 0:2, :])]
        l1 = load_list("l1", offs)
        xb_t.append(load("xb_23", [P, 2, D], F32, xb_p[:, 2:4, :]))
        xa_t.append(load("xa_23", [P, 2, D], F32, xa_p[:, 2:4, :]))
        so_t = load("so_t", [P, PACK, J], F32, planes(so))
        load_scales(nc.sync, w2_sraw, w2_scales, range(2))
        xo_01 = load("xo_01", [P, 2, 1024], F32, xo_p[:, 0:2, :])
        l3 = load_list("l3", offs3)
        fl_t = load_vec("fl_t", fl)
        load_scales(nc.sync, w2_sraw, w2_scales, range(2, 4))
        xo_2 = load("xo_2", [P, 1024], F32, xo_p[:, 2, :])
        w2_raw = load_words("w2_raw", w2_words[0].rearrange("p n t -> p (n t)"))
        xo_3 = load("xo_3", [P, 1024], F32, xo_p[:, 3, :])
        w_raw = load_words("w_raw", w_words[0].rearrange("p n t -> p (n t)"))
        xo_t = [xo_01[:, 0, :], xo_01[:, 1, :], xo_2[:], xo_3[:]]
        l4 = load_list("l4", offs4)
        tb_t = [load(f"tb{t}", [P, D], F32, tb_p[:, t, :]) for t in range(PACK)]
        wb_raw = load_words("wb_raw", wb_words[0])
        gm_t = load_vec("gm_t", gm)
        rs_t = load("rs_t", [P, PACK, J], F32, planes(rs))

        def deal(engine_copy, name, raw, dtype):
            dealt = pool.tile([P, D], dtype, name=name, align_bytes=64)
            engine_copy(
                out=dealt[:].rearrange("p (t m) -> p t m", t=PACK),
                in_=raw.rearrange("p (m t) -> p t m", t=PACK),
            )
            return dealt

        def by_word(ap):
            return ap.rearrange("p (c i) t -> p c t i", i=RUN)

        def by_plane(ap):
            return ap.rearrange("p t (c i) -> p c t i", i=RUN)

        def spread(vec):
            return vec[:].rearrange("p (c t i) -> p c t i", c=1, i=1).to_broadcast([P, HALF // RUN, PACK, RUN])

        def half(h):
            return slice(h * HALF, (h + 1) * HALF)

        def quantize(name, grouped, fmt):
            codes = pool.tile([P, HALF], U32, name=name + "_codes", align_bytes=64)
            scales = pool.tile([P, HALF], U8, name=name + "_scales", align_bytes=64)
            nc.vector.quantize_mx(out=codes[:].bitcast(fmt), scales=scales[:], in_=grouped.rearrange("p c t -> p (c t)"))
            return codes, scales

        def gather_s(dst, window, offsets):
            nc.scalar.activation(dst, window.indirect(offsets), COPY)

        def gather_v(dst, window, offsets):
            nc.vector.tensor_copy(dst, window.indirect(offsets))

        def half_list(lst, h):
            return lst[:, h * (HALF // 16) : (h + 1) * (HALF // 16)]

        fk_neg = pool.tile([P, PACK], F32, name="fk_neg", align_bytes=64)
        nc.scalar.activation(fk_neg[:], fk_t[:], COPY, scale=-1.0)
        xb_g = pool.tile([P, PACK, J], F32, name="xb_g")
        xa_g = pool.tile([P, PACK, J], F32, name="xa_g")
        gap = pool.tile([P, PACK, J], F32, name="gap")
        for pair in range(2):
            for dst, src, lst in ((xb_g, xb_t, l2), (xa_g, xa_t, l1)):
                gather_s(dst[:, 2 * pair, :], src[pair][:, 0, :], lst[:])
                gather_v(dst[:, 2 * pair + 1, :], src[pair][:, 1, :], lst[:])
            for t in (2 * pair + 1, 2 * pair):
                nc.vector.scalar_tensor_tensor(
                    gap[:, t, :], xb_g[:, t, :], hb_t[:, t : t + 1], xa_g[:, t, :], ALU.min, ALU.subtract
                )
        w_s = deal(nc.gpsimd.tensor_copy, "w_s", w_sraw[:], U8)
        w2_s = deal(nc.gpsimd.tensor_copy, "w2_s", w2_sraw[:], U8)
        wb_s = deal(nc.gpsimd.tensor_copy, "wb_s", wb_sraw[:], U8)
        u_b = [pool.tile([P, HALF, PACK], BF16, name=f"u_b{h}", align_bytes=64) for h in range(2)]
        for h in range(2):
            nc.vector.tensor_tensor(by_word(u_b[h][:]), by_plane(gap[:, :, half(h)]), spread(fk_neg), ALU.mult)
        u_q = [quantize(f"u_{h}", u_b[h][:], E5M2) for h in range(2)]
        acc = [psum.tile([P, PACK, HALF], F32, name=f"acc{h}") for h in range(2)]

        xo_g = pool.tile([P, PACK, J], F32, name="xo_g")
        m2 = pool.tile([P, PACK, J], F32, name="m2")
        u2_b = pool.tile([P, J, PACK], BF16, name="u2_b", align_bytes=64)

        def larger(t, cols):
            nc.vector.tensor_tensor(m2[:, t, cols], xo_g[:, t, cols], so_t[:, t, cols], ALU.max)

        def scaled(t, cols):
            nc.vector.tensor_scalar(u2_b[:, cols, t], m2[:, t, cols], fl_t[:, t : t + 1], None, ALU.mult)

        for t in range(PACK - 1):
            gather = gather_v if t == 1 else gather_s
            gather(xo_g[:, t, :], xo_t[t], l3[:])
        for t in (1, 0, 2):
            larger(t, slice(0, J))
            scaled(t, slice(0, J))
        w2_c = deal(nc.scalar.copy, "w2_c", w2_raw[:].bitcast(U32), U32)
        gather_v(xo_g[:, 3, half(0)], xo_t[3], half_list(l3, 0))
        gather_s(xo_g[:, 3, half(1)], xo_t[3], half_list(l3, 1))
        w_c = deal(nc.scalar.copy, "w_c", w_raw[:].bitcast(U32), U32)
        for h in range(2):
            codes, scales = u_q[h]
            for t in range(PACK):
                cols = slice(t * P, (t + 1) * P)
                nc.tensor.matmul_mx(
                    out=acc[h][:, t, :], lhsT=w_c[:, cols].bitcast(E5M2), lhsT_scale=w_s[:, cols],
                    rhs=codes[:].bitcast(E5M2), rhs_scale=scales[:], start=(t == 0), stop=False,
                )

        for h in range(2):
            larger(3, half(h))
        for h in range(2):
            scaled(3, half(h))
        for h in range(2):
            codes, scales = quantize(f"u2_{h}", u2_b[:, half(h), :], E5M2)
            for t in range(PACK):
                cols = slice(t * P, (t + 1) * P)
                nc.tensor.matmul_mx(
                    out=acc[h][:, t, :], lhsT=w2_c[:, cols].bitcast(E4M3), lhsT_scale=w2_s[:, cols],
                    rhs=codes[:].bitcast(E5M2), rhs_scale=scales[:], start=False, stop=(t == PACK - 1),
                )

        tb_g = pool.tile([P, PACK, J], F32, name="tb_g")
        for t in range(PACK - 1):
            gather = gather_v if t == 2 else gather_s
            gather(tb_g[:, t, :], tb_t[t][:], l4[:])
        for h in range(2):
            gather_s(tb_g[:, 3, half(h)], tb_t[3][:], half_list(l4, h))
        wb_c = deal(nc.scalar.copy, "wb_c", wb_raw[:].bitcast(U16), U16)
        hid_b = [pool.tile([P, HALF, PACK], BF16, name=f"hid_b{h}", align_bytes=64) for h in range(2)]
        res = [[psum.tile([P, 2, HALF], F32, name=f"res{h}{b}") for b in range(2)] for h in range(2)]
        for h in range(2):
            nc.vector.tensor_tensor(by_word(hid_b[h][:]), by_plane(acc[h][:]), by_plane(tb_g[:, :, half(h)]), ALU.max)
            codes, scales = quantize(f"hid_{h}", hid_b[h][:], E5M2)
            for t in range(PACK):
                cols = slice(t * P, (t + 1) * P)
                nc.tensor.matmul_mx(
                    out=res[h][t // 2][:, t % 2, :], lhsT=wb_c[:, cols].bitcast(E2M1), lhsT_scale=wb_s[:, cols],
                    rhs=codes[:].bitcast(E5M2), rhs_scale=scales[:], start=True, stop=True,
                )

        y_codes = pool.tile([P, J], U32, name="y_codes", align_bytes=64)
        y_scales = pool.tile([P, J], U8, name="y_scales", align_bytes=64)
        out_p = planes(out_0)
        words_out = out_1[0].rearrange("p c t -> p (c t)").bitcast(I32)
        y = [pool.tile([P, PACK, HALF], F32, name=f"y{h}") for h in range(2)]
        y_b = [pool.tile([P, HALF, PACK], BF16, name=f"y_b{h}", align_bytes=64) for h in range(2)]
        for h in range(2):
            for t in range(PACK):
                nc.vector.scalar_tensor_tensor(
                    y[h][:, t, :], res[h][t // 2][:, t % 2, :], gm_t[:, t : t + 1], rs_t[:, t, half(h)], ALU.mult, ALU.add
                )
            nc.sync.dma_start(out=out_p[:, :, half(h)], in_=y[h][:])
        nc.scalar.copy(out=by_word(y_b[0][:]), in_=by_plane(y[0][:]))
        for h in range(2):
            if h == 1:
                nc.vector.tensor_copy(out=by_word(y_b[1][:]), in_=by_plane(y[1][:]))
            nc.vector.quantize_mx(
                out=y_codes[:, half(h)].bitcast(E4M3), scales=y_scales[:, half(h)],
                in_=y_b[h][:].rearrange("p c t -> p (c t)"),
            )
            nc.scalar.dma_start(out=words_out[:, half(h)], in_=y_codes[:, half(h)].bitcast(I32))
        for q in range(4):
            queue = nc.sync if q % 2 == 0 else nc.scalar
            queue.dma_start(
                out=out_2[0, 4 * q : 4 * q + 4, :].bitcast(I32),
                in_=y_scales[32 * q : 32 * q + 4, :].bitcast(I32),
            )
